import numpy as np
import ml_dtypes


def mxq(x, axis, fmt="e4m3"):
    dtype, down = {"e4m3": (ml_dtypes.float8_e4m3fn, 7), "e5m2": (ml_dtypes.float8_e5m2, 14)}[fmt]
    v = np.moveaxis(np.asarray(x, np.float32).astype(ml_dtypes.bfloat16).astype(np.float64), axis, -1)
    blocks = v.reshape(v.shape[:-1] + (-1, 32))
    amax = np.abs(blocks).max(-1, keepdims=True)
    byte = np.maximum(np.where(amax > 0, np.frexp(amax)[1] - 1 + 127, 0) - down, 1)
    scale = np.exp2(byte - 127.0)
    codes = (blocks / scale).astype(np.float32).astype(dtype).astype(np.float64)
    return np.moveaxis((codes * scale).reshape(v.shape), -1, axis)


WIDE = False


def mx_kscale(k):
    if not WIDE:
        return np.ones(k)
    levels = np.array([10, -10, 5, -5, 0])
    if k % 512:
        return np.exp2(np.random.permutation(np.resize(levels, k // 32))).repeat(32)
    a = np.empty((k // 512, 16))
    for p in range(k // 512):
        a[p, :8] = np.random.permutation(np.resize(levels, 8))
        for g in range(8):
            far = levels[np.abs(levels - a[p, g]) >= 10]
            a[p, g + 8] = far[np.random.randint(len(far))]
    return np.exp2(a.ravel()).repeat(32)


def f64(x):
    return np.asarray(x).astype(np.float64)


def striped(idx):
    return np.tile(idx.reshape(-1, 16).T, (8, 1)).astype(np.uint16)


def unstriped(offs):
    return offs[:16].T.reshape(-1).astype(np.int64)


def silu(v):
    return v / (1.0 + np.exp(-np.maximum(v, -700.0)))


K, T, S, V, H, N, J = 512, 2048, 1024, 512, 512, 256, 512


def setup_inputs():
    n = np.random.standard_normal
    s = mx_kscale(K)[:, None]
    u = mx_kscale(H)
    r = mx_kscale(J)[:, None]
    return {
        "xT": (n((K, T)) * s).astype(np.float32),
        "eT": (n((J, V)) * r).astype(np.float32),
        "w1": (n((K, H)) / np.sqrt(3 * K) / s * u).astype(np.float32),
        "w2": (n((K, H)) / np.sqrt(3 * K) / s * u).astype(np.float32),
        "w3": (n((J, H)) / np.sqrt(3 * J) / r * u).astype(np.float32),
        "w4": (n((H, N)) / np.sqrt(H) / u[:, None]).astype(np.float32),
        "offs": striped(np.random.permutation(T)[:S]),
    }


def reference(xT, eT, w1, w2, w3, w4, offs):
    xq = mxq(f64(xT)[:, unstriped(offs)], 0, "e4m3")
    h = silu(mxq(f64(w1), 0, "e4m3").T @ xq[:, :V] + mxq(f64(w2), 0, "e4m3").T @ xq[:, V:2 * V] + mxq(f64(w3), 0, "e4m3").T @ mxq(f64(eT), 0, "e4m3"))
    return mxq(f64(w4), 0, "e4m3").T @ mxq(h, 0, "e4m3")

@@ -1,0 +1,165 @@
+from contextlib import ExitStack
+
+import concourse.mybir as mybir
+
+K, T, S, V, H, N = 512, 2048, 1024, 512, 512, 256
+FLOPS = 2 * V * (3 * K * H + H * N)
+
+F32 = mybir.dt.float32
+BF16 = mybir.dt.bfloat16
+U32 = mybir.dt.uint32
+U16 = mybir.dt.uint16
+U8 = mybir.dt.uint8
+FP8X4 = mybir.dt.float8_e4m3fn_x4
+COPY = mybir.ActivationFunctionType.Copy
+SILU = mybir.ActivationFunctionType.Silu
+
+P = 128
+PACK = 4
+CH = 128
+NCH = V // CH
+HALF = T // 2
+
+
+def tile_picked_edgeup_silu_e_kernel(tc, xT, eT, w1, w2, w3, w4, offs, out):
+    nc = tc.nc
+    with ExitStack() as ctx:
+        sb = ctx.enter_context(tc.tile_pool(name="sb", bufs=1))
+        ps = ctx.enter_context(tc.psum_pool(name="ps", bufs=1))
+
+        def cast(engine, dst, src):
+            if engine == "vector":
+                nc.vector.tensor_copy(out=dst, in_=src)
+            else:
+                nc.scalar.activation(out=dst, in_=src, func=COPY)
+
+        def quantize(name, grouped, width):
+            codes = sb.tile([P, width], U32, name=name + "_codes", align_bytes=64)
+            scales = sb.tile([P, width], U8, name=name + "_scales", align_bytes=64)
+            nc.vector.quantize_mx(out=codes[:].bitcast(FP8X4), scales=scales[:], in_=grouped)
+            return codes, scales
+
+        warm_in = sb.tile([P, 8], F32, name="warm_in")
+        warm_out = sb.tile([P, 8], F32, name="warm_out")
+        nc.gpsimd.memset(warm_in[:], 0.0)
+        nc.scalar.activation(out=warm_out[:], in_=warm_in[:], func=SILU)
+
+        x_rows = xT.rearrange("(p u e) t -> p u e t", u=2, e=2)
+        x_raw = {}
+        offsets = sb.tile([P, S // 16], U16, name="offsets")
+        for u in range(2):
+            for a in range(2):
+                x_raw[u, a] = sb.tile([P, 2, HALF], F32, name=f"x_raw{u}{a}")
+                nc.sync.dma_start(out=x_raw[u, a][:], in_=x_rows[:, u, :, a * HALF:(a + 1) * HALF])
+                if u == 0 and a == 0:
+                    nc.sync.dma_start(offsets[:], offs)
+        w_raw = []
+        for i, w in enumerate((w1, w2, w3)):
+            w_raw.append(sb.tile([P, PACK, H], F32, name=f"w_raw{i}"))
+            nc.sync.dma_start(out=w_raw[i][:], in_=w.rearrange("(p j) c -> p j c", j=PACK))
+        e_rows = eT.rearrange("(p j) v -> p j v", j=PACK)
+        e_raw = []
+        for a in range(2):
+            e_raw.append(sb.tile([P, PACK, V // 2], F32, name=f"e_raw{a}"))
+            nc.sync.dma_start(out=e_raw[a][:], in_=e_rows[:, :, a * (V // 2):(a + 1) * (V // 2)])
+        w4_raw = sb.tile([P, PACK, N], F32, name="w4_raw")
+        nc.sync.dma_start(out=w4_raw[:], in_=w4.rearrange("(p j) n -> p j n", j=PACK))
+
+        picked = sb.tile([P, S, 2], U32, name="picked", align_bytes=64)
+        X_SPLIT = 704
+        for u in range(2):
+            pairs = sb.tile([P, T], U32, name=f"pairs{u}")
+            pv = pairs[:].bitcast(BF16).rearrange("p (t e) -> p t e", e=2)
+            for a in range(2):
+                parts = (("scalar", 0, HALF),) if a == 0 else (("vector", 0, X_SPLIT), ("scalar", X_SPLIT, HALF))
+                for engine, lo, hi in parts:
+                    cast(engine,
+                         pv[:, a * HALF + lo:a * HALF + hi, :].rearrange("p (c i) e -> p c e i", i=4),
+                         x_raw[u, a][:, :, lo:hi].rearrange("p e (c i) -> p c e i", i=4))
+            if u == 0:
+                nc.vector.tensor_copy(out=picked[:, :, u], in_=pairs[:].indirect(offsets[:]))
+            else:
+                for d in range(2):
+                    nc.vector.tensor_copy(out=picked[:, d * V:(d + 1) * V, u],
+                                          in_=pairs[:].indirect(offsets[:, d * V // 16:(d + 1) * V // 16]))
+        picked_bf = picked[:].rearrange("p s u -> p (s u)").bitcast(BF16)
+        x_q = [quantize(f"x{d}", picked_bf[:, d * PACK * V:(d + 1) * PACK * V], V) for d in range(2)]
+
+        w_q = []
+        for i in range(3):
+            src = w_raw[i][:].rearrange("p j (m t) -> p m j t", t=PACK)
+            if i == 0:
+                parts = (("scalar", 0, 4),)
+            else:
+                parts = (("scalar", 2, 4), ("vector", 0, 2))
+            grouped = {}
+            for engine, lo, hi in parts:
+                grouped[lo] = sb.tile([P, hi - lo, P, PACK], BF16, name=f"w_grouped{i}{lo}", align_bytes=64)
+                cast(engine, grouped[lo][:].rearrange("p t m j -> p m j t"), src[:, :, :, lo:hi])
+            tiles = []
+            for engine, lo, hi in sorted(parts, key=lambda part: part[1]):
+                q = quantize(f"w{i}{lo}", grouped[lo][:].rearrange("p t m j -> p (t m j)"), (hi - lo) * P)
+                tiles.extend((q[0][:, t * P:(t + 1) * P], q[1][:, t * P:(t + 1) * P]) for t in range(hi - lo))
+            w_q.append(tiles)
+
+        e_q = {}
+
+        def edge_features(c):
+            grouped = sb.tile([P, CH, PACK], BF16, name=f"e_grouped{c}", align_bytes=64)
+            lo = (c % 2) * CH
+            cast("scalar" if c < 2 else "vector",
+                 grouped[:].rearrange("p (c i) t -> p c t i", i=4),
+                 e_raw[c // 2][:, :, lo:lo + CH].rearrange("p t (c i) -> p c t i", i=4))
+            e_q[c] = quantize(f"e{c}", grouped[:].rearrange("p c t -> p (c t)"), CH)
+
+        h_bf = {}
+        acc = {}
+        per_bank = (2, 2, 4, 4)
+
+        def mx_pass(c, t, i):
+            cols = slice(c * CH, (c + 1) * CH)
+            codes, scales = (x_q[i][0][:, cols], x_q[i][1][:, cols]) if i < 2 else (e_q[c][0][:], e_q[c][1][:])
+            first = t - t % per_bank[c]
+            nc.tensor.matmul_mx(out=acc[c, first][:, t - first, :], lhsT=w_q[i][t][0].bitcast(FP8X4),
+                                lhsT_scale=w_q[i][t][1], rhs=codes.bitcast(FP8X4), rhs_scale=scales,
+                                start=(i == 0), stop=(i == 2))
+
+        for c in range(NCH):
+            for first in range(0, PACK, per_bank[c]):
+                acc[c, first] = ps.tile([P, per_bank[c], CH], F32, name=f"acc{c}{first}", tag=f"bank{len(acc)}")
+        for i in range(2):
+            for c, first in acc:
+                mx_pass(c, first, i)
+
+        def layer1(c):
+            h_bf[c] = sb.tile([P, CH, PACK], BF16, name=f"h{c}", align_bytes=64)
+            for first in range(0, PACK, per_bank[c]):
+                mx_pass(c, first, 2)
+                for t in range(first + 1, first + per_bank[c]):
+                    for i in range(3):
+                        mx_pass(c, t, i)
+                nc.scalar.activation(out=h_bf[c][:, :, first:first + per_bank[c]],
+                                     in_=acc[c, first][:].rearrange("p t v -> p v t"), func=SILU)
+
+        out_rows = out.rearrange("(a p) v -> p a v", p=P)
+
+        def layer2(c, w4_q):
+            h_q = quantize(f"h{c}", h_bf[c][:].rearrange("p v t -> p (v t)"), CH)
+            res = ps.tile([P, 2, CH], F32, name=f"res{c}", tag=f"bank{(6 + c) % 8}")
+            for a in range(2):
+                nc.tensor.matmul_mx(out=res[:, a, :], lhsT=w4_q[0][:, a * P:(a + 1) * P].bitcast(FP8X4),
+                                    lhsT_scale=w4_q[1][:, a * P:(a + 1) * P],
+                                    rhs=h_q[0][:].bitcast(FP8X4), rhs_scale=h_q[1][:], start=True, stop=True)
+            staged = sb.tile([P, 2, CH], F32, name=f"staged{c}")
+            cast("scalar" if c == 2 else "vector", staged[:], res[:])
+            nc.sync.dma_start(out=out_rows[:, :, c * CH:(c + 1) * CH], in_=staged[:])
+
+        for c in range(NCH):
+            edge_features(c)
+            layer1(c)
+        w4_grouped = sb.tile([P, N, PACK], BF16, name="w4_grouped", align_bytes=64)
+        cast("vector", w4_grouped[:].rearrange("p (c i) t -> p c t i", i=4),
+             w4_raw[:].rearrange("p t (c i) -> p c t i", i=4))
+        w4_q = quantize("w4", w4_grouped[:].rearrange("p c t -> p (c t)"), N)
+        for c in range(NCH):
+            layer2(c, w4_q)

@@ -18,7 +18,9 @@ P = 128
 PACK = 4
 CH = 128
 NCH = V // CH
-HALF = T // 2
+SPANS = ((0, 256), (256, 384), (384, 512))
+X_PIECES = ((0, 1024), (1024, 1536), (1536, 2048))
+X_ON_SCALAR = ((768, 0, 160), (896, 0, 160))
 
 
 def tile_picked_edgeup_silu_e_kernel(tc, xT, eT, w1, w2, w3, w4, offs, out):
@@ -48,34 +50,39 @@ def tile_picked_edgeup_silu_e_kernel(tc, xT, eT, w1, w2, w3, w4, offs, out):
         x_raw = {}
         offsets = sb.tile([P, S // 16], U16, name="offsets")
         for u in range(2):
-            for a in range(2):
-                x_raw[u, a] = sb.tile([P, 2, HALF], F32, name=f"x_raw{u}{a}")
-                nc.sync.dma_start(out=x_raw[u, a][:], in_=x_rows[:, u, :, a * HALF:(a + 1) * HALF])
-                if u == 0 and a == 0:
+            for lo, hi in X_PIECES:
+                x_raw[u, lo] = sb.tile([P, 2, hi - lo], F32, name=f"x_raw{u}_{lo}")
+                nc.sync.dma_start(out=x_raw[u, lo][:], in_=x_rows[:, u, :, lo:hi])
+                if u == 0 and lo == 0:
                     nc.sync.dma_start(offsets[:], offs)
-        w_raw = []
-        for i, w in enumerate((w1, w2, w3)):
-            w_raw.append(sb.tile([P, PACK, H], F32, name=f"w_raw{i}"))
-            nc.sync.dma_start(out=w_raw[i][:], in_=w.rearrange("(p j) c -> p j c", j=PACK))
+        w_raw = [sb.tile([P, PACK, H], F32, name=f"w_raw{i}") for i in range(3)]
+        e_raw = [sb.tile([P, PACK, hi - lo], F32, name=f"e_raw{lo}") for lo, hi in SPANS]
         e_rows = eT.rearrange("(p j) v -> p j v", j=PACK)
-        e_raw = []
-        for a in range(2):
-            e_raw.append(sb.tile([P, PACK, V // 2], F32, name=f"e_raw{a}"))
-            nc.sync.dma_start(out=e_raw[a][:], in_=e_rows[:, :, a * (V // 2):(a + 1) * (V // 2)])
+
+        def load_w(i):
+            nc.sync.dma_start(out=w_raw[i][:], in_=(w1, w2, w3)[i].rearrange("(p j) c -> p j c", j=PACK))
+
+        def load_e(n):
+            nc.sync.dma_start(out=e_raw[n][:], in_=e_rows[:, :, SPANS[n][0]:SPANS[n][1]])
+
+        load_w(0)
+        load_w(1)
+        load_e(0)
+        load_w(2)
+        load_e(1)
+        load_e(2)
         w4_raw = sb.tile([P, PACK, N], F32, name="w4_raw")
         nc.sync.dma_start(out=w4_raw[:], in_=w4.rearrange("(p j) n -> p j n", j=PACK))
 
         picked = sb.tile([P, S, 2], U32, name="picked", align_bytes=64)
-        X_SPLIT = 704
         for u in range(2):
             pairs = sb.tile([P, T], U32, name=f"pairs{u}")
             pv = pairs[:].bitcast(BF16).rearrange("p (t e) -> p t e", e=2)
-            for a in range(2):
-                parts = (("scalar", 0, HALF),) if a == 0 else (("vector", 0, X_SPLIT), ("scalar", X_SPLIT, HALF))
-                for engine, lo, hi in parts:
-                    cast(engine,
-                         pv[:, a * HALF + lo:a * HALF + hi, :].rearrange("p (c i) e -> p c e i", i=4),
-                         x_raw[u, a][:, :, lo:hi].rearrange("p e (c i) -> p c e i", i=4))
+            for (lo, hi), on_scalar in zip(X_PIECES, X_ON_SCALAR[u]):
+                for engine, a, b in (("scalar", lo, lo + on_scalar), ("vector", lo + on_scalar, hi)):
+                    if b > a:
+                        cast(engine, pv[:, a:b, :].rearrange("p (c i) e -> p c e i", i=4),
+                             x_raw[u, lo][:, :, a - lo:b - lo].rearrange("p e (c i) -> p c e i", i=4))
             if u == 0:
                 nc.vector.tensor_copy(out=picked[:, :, u], in_=pairs[:].indirect(offsets[:]))
             else:
@@ -85,81 +92,79 @@ def tile_picked_edgeup_silu_e_kernel(tc, xT, eT, w1, w2, w3, w4, offs, out):
         picked_bf = picked[:].rearrange("p s u -> p (s u)").bitcast(BF16)
         x_q = [quantize(f"x{d}", picked_bf[:, d * PACK * V:(d + 1) * PACK * V], V) for d in range(2)]
 
-        w_q = []
-        for i in range(3):
+        w_q = {}
+
+        def weights(i, parts):
             src = w_raw[i][:].rearrange("p j (m t) -> p m j t", t=PACK)
-            if i == 0:
-                parts = (("scalar", 0, 4),)
-            else:
-                parts = (("scalar", 2, 4), ("vector", 0, 2))
-            grouped = {}
             for engine, lo, hi in parts:
-                grouped[lo] = sb.tile([P, hi - lo, P, PACK], BF16, name=f"w_grouped{i}{lo}", align_bytes=64)
-                cast(engine, grouped[lo][:].rearrange("p t m j -> p m j t"), src[:, :, :, lo:hi])
-            tiles = []
-            for engine, lo, hi in sorted(parts, key=lambda part: part[1]):
-                q = quantize(f"w{i}{lo}", grouped[lo][:].rearrange("p t m j -> p (t m j)"), (hi - lo) * P)
-                tiles.extend((q[0][:, t * P:(t + 1) * P], q[1][:, t * P:(t + 1) * P]) for t in range(hi - lo))
-            w_q.append(tiles)
+                grouped = sb.tile([P, hi - lo, P, PACK], BF16, name=f"w_grouped{i}{lo}", align_bytes=64)
+                cast(engine, grouped[:].rearrange("p t m j -> p m j t"), src[:, :, :, lo:hi])
+                q = quantize(f"w{i}{lo}", grouped[:].rearrange("p t m j -> p (t m j)"), (hi - lo) * P)
+                for t in range(lo, hi):
+                    cols = slice((t - lo) * P, (t - lo + 1) * P)
+                    w_q[i, t] = (q[0][:, cols], q[1][:, cols])
 
         e_q = {}
 
-        def edge_features(c):
-            grouped = sb.tile([P, CH, PACK], BF16, name=f"e_grouped{c}", align_bytes=64)
-            lo = (c % 2) * CH
-            cast("scalar" if c < 2 else "vector",
-                 grouped[:].rearrange("p (c i) t -> p c t i", i=4),
-                 e_raw[c // 2][:, :, lo:lo + CH].rearrange("p t (c i) -> p c t i", i=4))
-            e_q[c] = quantize(f"e{c}", grouped[:].rearrange("p c t -> p (c t)"), CH)
+        def edge_features(n, engine):
+            width = SPANS[n][1] - SPANS[n][0]
+            grouped = sb.tile([P, width, PACK], BF16, name=f"e_grouped{n}", align_bytes=64)
+            cast(engine, grouped[:].rearrange("p (c i) t -> p c t i", i=4),
+                 e_raw[n][:].rearrange("p t (c i) -> p c t i", i=4))
+            e_q[n] = quantize(f"e{n}", grouped[:].rearrange("p c t -> p (c t)"), width)
 
-        h_bf = {}
-        acc = {}
-        per_bank = (2, 2, 4, 4)
+        def mx_pass(acc, n, t, i, start):
+            cols = slice(SPANS[n][0], SPANS[n][1])
+            codes, scales = (x_q[i][0][:, cols], x_q[i][1][:, cols]) if i < 2 else (e_q[n][0][:], e_q[n][1][:])
+            nc.tensor.matmul_mx(out=acc, lhsT=w_q[i, t][0].bitcast(FP8X4), lhsT_scale=w_q[i, t][1],
+                                rhs=codes.bitcast(FP8X4), rhs_scale=scales, start=start, stop=(i == 2))
 
-        def mx_pass(c, t, i):
-            cols = slice(c * CH, (c + 1) * CH)
-            codes, scales = (x_q[i][0][:, cols], x_q[i][1][:, cols]) if i < 2 else (e_q[c][0][:], e_q[c][1][:])
-            first = t - t % per_bank[c]
-            nc.tensor.matmul_mx(out=acc[c, first][:, t - first, :], lhsT=w_q[i][t][0].bitcast(FP8X4),
-                                lhsT_scale=w_q[i][t][1], rhs=codes.bitcast(FP8X4), rhs_scale=scales,
-                                start=(i == 0), stop=(i == 2))
+        weights(0, (("scalar", 0, 4),))
+        weights(1, (("scalar", 0, 2), ("scalar", 2, 4)))
+        edge_features(0, "vector")
 
-        for c in range(NCH):
-            for first in range(0, PACK, per_bank[c]):
-                acc[c, first] = ps.tile([P, per_bank[c], CH], F32, name=f"acc{c}{first}", tag=f"bank{len(acc)}")
-        for i in range(2):
-            for c, first in acc:
-                mx_pass(c, first, i)
+        wide = [ps.tile([P, SPANS[0][1]], F32, name=f"wide{t}", tag=f"bank{t}") for t in range(PACK)]
+        narrow = {n: ps.tile([P, PACK, CH], F32, name=f"narrow{n}", tag=f"bank{3 + n}") for n in (1, 2)}
+        ahead = [(wide[0][:], 0, 0), (wide[1][:], 0, 1), (narrow[1][:, 0, :], 1, 0), (narrow[2][:, 0, :], 2, 0),
+                 (wide[2][:], 0, 2), (wide[3][:], 0, 3)]
+        for acc, n, t in ahead:
+            mx_pass(acc, n, t, 1, True)
+            mx_pass(acc, n, t, 0, False)
 
-        def layer1(c):
-            h_bf[c] = sb.tile([P, CH, PACK], BF16, name=f"h{c}", align_bytes=64)
-            for first in range(0, PACK, per_bank[c]):
-                mx_pass(c, first, 2)
-                for t in range(first + 1, first + per_bank[c]):
-                    for i in range(3):
-                        mx_pass(c, t, i)
-                nc.scalar.activation(out=h_bf[c][:, :, first:first + per_bank[c]],
-                                     in_=acc[c, first][:].rearrange("p t v -> p v t"), func=SILU)
+        weights(2, (("vector", 0, 2), ("scalar", 2, 4)))
+        edge_features(1, "vector")
+        edge_features(2, "vector")
 
-        out_rows = out.rearrange("(a p) v -> p a v", p=P)
+        h_span = [sb.tile([P, hi - lo, PACK], BF16, name=f"h{lo}", align_bytes=64) for lo, hi in SPANS]
+        h_planes = sb.tile([P, PACK, SPANS[0][1]], BF16, name="h_planes")
+        for t in range(PACK):
+            mx_pass(wide[t][:], 0, t, 2, False)
+            nc.scalar.activation(out=h_planes[:, t, :], in_=wide[t][:], func=SILU)
+        for n in (1, 2):
+            mx_pass(narrow[n][:, 0, :], n, 0, 2, False)
+            for t in range(1, PACK):
+                for i in range(3):
+                    mx_pass(narrow[n][:, t, :], n, t, i, i == 0)
+            nc.scalar.activation(out=h_span[n][:], in_=narrow[n][:].rearrange("p t v -> p v t"), func=SILU)
 
-        def layer2(c, w4_q):
-            h_q = quantize(f"h{c}", h_bf[c][:].rearrange("p v t -> p (v t)"), CH)
-            res = ps.tile([P, 2, CH], F32, name=f"res{c}", tag=f"bank{(6 + c) % 8}")
-            for a in range(2):
-                nc.tensor.matmul_mx(out=res[:, a, :], lhsT=w4_q[0][:, a * P:(a + 1) * P].bitcast(FP8X4),
-                                    lhsT_scale=w4_q[1][:, a * P:(a + 1) * P],
-                                    rhs=h_q[0][:].bitcast(FP8X4), rhs_scale=h_q[1][:], start=True, stop=True)
-            staged = sb.tile([P, 2, CH], F32, name=f"staged{c}")
-            cast("scalar" if c == 2 else "vector", staged[:], res[:])
-            nc.sync.dma_start(out=out_rows[:, :, c * CH:(c + 1) * CH], in_=staged[:])
-
-        for c in range(NCH):
-            edge_features(c)
-            layer1(c)
         w4_grouped = sb.tile([P, N, PACK], BF16, name="w4_grouped", align_bytes=64)
         cast("vector", w4_grouped[:].rearrange("p (c i) t -> p c t i", i=4),
              w4_raw[:].rearrange("p t (c i) -> p c t i", i=4))
         w4_q = quantize("w4", w4_grouped[:].rearrange("p c t -> p (c t)"), N)
-        for c in range(NCH):
-            layer2(c, w4_q)
+        nc.vector.tensor_copy(out=h_span[0][:].rearrange("p (c i) t -> p c t i", i=4),
+                              in_=h_planes[:].rearrange("p t (c i) -> p c t i", i=4))
+
+        out_rows = out.rearrange("(a p) v -> p a v", p=P)
+        for n, (lo, hi) in enumerate(SPANS):
+            width = hi - lo
+            h_q = quantize(f"h{lo}", h_span[n][:].rearrange("p v t -> p (v t)"), width)
+            groups = (((0, 1, 6, "vector"), (1, 2, 7, "scalar")), ((0, 2, 1, "scalar"),), ((0, 2, 0, "vector"),))[n]
+            for a0, a1, bank, engine in groups:
+                res = ps.tile([P, a1 - a0, width], F32, name=f"res{lo}_{a0}", tag=f"bank{bank}")
+                for a in range(a0, a1):
+                    nc.tensor.matmul_mx(out=res[:, a - a0, :], lhsT=w4_q[0][:, a * P:(a + 1) * P].bitcast(FP8X4),
+                                        lhsT_scale=w4_q[1][:, a * P:(a + 1) * P],
+                                        rhs=h_q[0][:].bitcast(FP8X4), rhs_scale=h_q[1][:], start=True, stop=True)
+                staged = sb.tile([P, a1 - a0, width], F32, name=f"staged{lo}_{a0}")
+                cast(engine, staged[:], res[:])
+                nc.sync.dma_start(out=out_rows[:, a0:a1, lo:hi], in_=staged[:])

@@ -8,6 +8,7 @@ FLOPS = 2 * V * (3 * K * H + H * N)
 F32 = mybir.dt.float32
 BF16 = mybir.dt.bfloat16
 U32 = mybir.dt.uint32
+I32 = mybir.dt.int32
 U16 = mybir.dt.uint16
 U8 = mybir.dt.uint8
 FP8X4 = mybir.dt.float8_e4m3fn_x4
@@ -74,7 +75,7 @@ def tile_picked_edgeup_silu_e_kernel(tc, xT, eT, w1, w2, w3, w4, offs, out):
         w4_raw = sb.tile([P, PACK, N], F32, name="w4_raw")
         nc.sync.dma_start(out=w4_raw[:], in_=w4.rearrange("(p j) n -> p j n", j=PACK))
 
-        picked = sb.tile([P, S, 2], U32, name="picked", align_bytes=64)
+        gathered = [sb.tile([P, 2, V], U32, name=f"gathered{d}") for d in range(2)]
         for u in range(2):
             pairs = sb.tile([P, T], U32, name=f"pairs{u}")
             pv = pairs[:].bitcast(BF16).rearrange("p (t e) -> p t e", e=2)
@@ -83,14 +84,13 @@ def tile_picked_edgeup_silu_e_kernel(tc, xT, eT, w1, w2, w3, w4, offs, out):
                     if b > a:
                         cast(engine, pv[:, a:b, :].rearrange("p (c i) e -> p c e i", i=4),
                              x_raw[u, lo][:, :, a - lo:b - lo].rearrange("p e (c i) -> p c e i", i=4))
-            if u == 0:
-                nc.vector.tensor_copy(out=picked[:, :, u], in_=pairs[:].indirect(offsets[:]))
-            else:
-                for d in range(2):
-                    nc.vector.tensor_copy(out=picked[:, d * V:(d + 1) * V, u],
-                                          in_=pairs[:].indirect(offsets[:, d * V // 16:(d + 1) * V // 16]))
-        picked_bf = picked[:].rearrange("p s u -> p (s u)").bitcast(BF16)
-        x_q = [quantize(f"x{d}", picked_bf[:, d * PACK * V:(d + 1) * PACK * V], V) for d in range(2)]
+            for d in range(2):
+                nc.vector.tensor_copy(out=gathered[d][:, u, :],
+                                      in_=pairs[:].indirect(offsets[:, d * V // 16:(d + 1) * V // 16]))
+        picked = [sb.tile([P, V, 2], I32, name=f"picked{d}", align_bytes=64) for d in range(2)]
+        for d in range(2):
+            nc.vector.tensor_copy(out=picked[d][:], in_=gathered[d][:].bitcast(I32).rearrange("p u v -> p v u"))
+        x_q = [quantize(f"x{d}", picked[d][:].rearrange("p v u -> p (v u)").bitcast(BF16), V) for d in range(2)]
 
         w_q = {}
 

from contextlib import ExitStack

import concourse.mybir as mybir

K, T, S, V, H, N = 512, 2048, 1024, 512, 512, 256
FLOPS = 2 * V * (3 * K * H + H * N)

F32 = mybir.dt.float32
BF16 = mybir.dt.bfloat16
U32 = mybir.dt.uint32
I32 = mybir.dt.int32
U16 = mybir.dt.uint16
U8 = mybir.dt.uint8
FP8X4 = mybir.dt.float8_e4m3fn_x4
COPY = mybir.ActivationFunctionType.Copy
SILU = mybir.ActivationFunctionType.Silu

P = 128
PACK = 4
CH = 128
NCH = V // CH
SPANS = ((0, 256), (256, 384), (384, 512))
X_PIECES = ((0, 1024), (1024, 1536), (1536, 2048))
X_ON_SCALAR = ((768, 0, 160), (896, 0, 160))


def tile_picked_edgeup_silu_e_kernel(tc, xT, eT, w1, w2, w3, w4, offs, out):
    nc = tc.nc
    with ExitStack() as ctx:
        sb = ctx.enter_context(tc.tile_pool(name="sb", bufs=1))
        ps = ctx.enter_context(tc.psum_pool(name="ps", bufs=1))

        def cast(engine, dst, src):
            if engine == "vector":
                nc.vector.tensor_copy(out=dst, in_=src)
            else:
                nc.scalar.activation(out=dst, in_=src, func=COPY)

        def quantize(name, grouped, width):
            codes = sb.tile([P, width], U32, name=name + "_codes", align_bytes=64)
            scales = sb.tile([P, width], U8, name=name + "_scales", align_bytes=64)
            nc.vector.quantize_mx(out=codes[:].bitcast(FP8X4), scales=scales[:], in_=grouped)
            return codes, scales

        warm_in = sb.tile([P, 8], F32, name="warm_in")
        warm_out = sb.tile([P, 8], F32, name="warm_out")
        nc.gpsimd.memset(warm_in[:], 0.0)
        nc.scalar.activation(out=warm_out[:], in_=warm_in[:], func=SILU)

        x_rows = xT.rearrange("(p u e) t -> p u e t", u=2, e=2)
        x_raw = {}
        offsets = sb.tile([P, S // 16], U16, name="offsets")
        for u in range(2):
            for lo, hi in X_PIECES:
                x_raw[u, lo] = sb.tile([P, 2, hi - lo], F32, name=f"x_raw{u}_{lo}")
                nc.sync.dma_start(out=x_raw[u, lo][:], in_=x_rows[:, u, :, lo:hi])
                if u == 0 and lo == 0:
                    nc.sync.dma_start(offsets[:], offs)
        w_raw = [sb.tile([P, PACK, H], F32, name=f"w_raw{i}") for i in range(3)]
        e_raw = [sb.tile([P, PACK, hi - lo], F32, name=f"e_raw{lo}") for lo, hi in SPANS]
        e_rows = eT.rearrange("(p j) v -> p j v", j=PACK)

        def load_w(i):
            nc.sync.dma_start(out=w_raw[i][:], in_=(w1, w2, w3)[i].rearrange("(p j) c -> p j c", j=PACK))

        def load_e(n):
            nc.sync.dma_start(out=e_raw[n][:], in_=e_rows[:, :, SPANS[n][0]:SPANS[n][1]])

        load_w(0)
        load_w(1)
        load_e(0)
        load_w(2)
        load_e(1)
        load_e(2)
        w4_raw = sb.tile([P, PACK, N], F32, name="w4_raw")
        nc.sync.dma_start(out=w4_raw[:], in_=w4.rearrange("(p j) n -> p j n", j=PACK))

        gathered = [sb.tile([P, 2, V], U32, name=f"gathered{d}") for d in range(2)]
        for u in range(2):
            pairs = sb.tile([P, T], U32, name=f"pairs{u}")
            pv = pairs[:].bitcast(BF16).rearrange("p (t e) -> p t e", e=2)
            for (lo, hi), on_scalar in zip(X_PIECES, X_ON_SCALAR[u]):
                for engine, a, b in (("scalar", lo, lo + on_scalar), ("vector", lo + on_scalar, hi)):
                    if b > a:
                        cast(engine, pv[:, a:b, :].rearrange("p (c i) e -> p c e i", i=4),
                             x_raw[u, lo][:, :, a - lo:b - lo].rearrange("p e (c i) -> p c e i", i=4))
            for d in range(2):
                nc.vector.tensor_copy(out=gathered[d][:, u, :],
                                      in_=pairs[:].indirect(offsets[:, d * V // 16:(d + 1) * V // 16]))
        picked = [sb.tile([P, V, 2], I32, name=f"picked{d}", align_bytes=64) for d in range(2)]
        for d in range(2):
            nc.vector.tensor_copy(out=picked[d][:], in_=gathered[d][:].bitcast(I32).rearrange("p u v -> p v u"))
        x_q = [quantize(f"x{d}", picked[d][:].rearrange("p v u -> p (v u)").bitcast(BF16), V) for d in range(2)]

        w_q = {}

        def weights(i, parts):
            src = w_raw[i][:].rearrange("p j (m t) -> p m j t", t=PACK)
            for engine, lo, hi in parts:
                grouped = sb.tile([P, hi - lo, P, PACK], BF16, name=f"w_grouped{i}{lo}", align_bytes=64)
                cast(engine, grouped[:].rearrange("p t m j -> p m j t"), src[:, :, :, lo:hi])
                q = quantize(f"w{i}{lo}", grouped[:].rearrange("p t m j -> p (t m j)"), (hi - lo) * P)
                for t in range(lo, hi):
                    cols = slice((t - lo) * P, (t - lo + 1) * P)
                    w_q[i, t] = (q[0][:, cols], q[1][:, cols])

        e_q = {}

        def edge_features(n, engine):
            width = SPANS[n][1] - SPANS[n][0]
            grouped = sb.tile([P, width, PACK], BF16, name=f"e_grouped{n}", align_bytes=64)
            cast(engine, grouped[:].rearrange("p (c i) t -> p c t i", i=4),
                 e_raw[n][:].rearrange("p t (c i) -> p c t i", i=4))
            e_q[n] = quantize(f"e{n}", grouped[:].rearrange("p c t -> p (c t)"), width)

        def mx_pass(acc, n, t, i, start):
            cols = slice(SPANS[n][0], SPANS[n][1])
            codes, scales = (x_q[i][0][:, cols], x_q[i][1][:, cols]) if i < 2 else (e_q[n][0][:], e_q[n][1][:])
            nc.tensor.matmul_mx(out=acc, lhsT=w_q[i, t][0].bitcast(FP8X4), lhsT_scale=w_q[i, t][1],
                                rhs=codes.bitcast(FP8X4), rhs_scale=scales, start=start, stop=(i == 2))

        weights(0, (("scalar", 0, 4),))
        weights(1, (("scalar", 0, 2), ("scalar", 2, 4)))
        edge_features(0, "vector")

        wide = [ps.tile([P, SPANS[0][1]], F32, name=f"wide{t}", tag=f"bank{t}") for t in range(PACK)]
        narrow = {n: ps.tile([P, PACK, CH], F32, name=f"narrow{n}", tag=f"bank{3 + n}") for n in (1, 2)}
        ahead = [(wide[0][:], 0, 0), (wide[1][:], 0, 1), (narrow[1][:, 0, :], 1, 0), (narrow[2][:, 0, :], 2, 0),
                 (wide[2][:], 0, 2), (wide[3][:], 0, 3)]
        for acc, n, t in ahead:
            mx_pass(acc, n, t, 1, True)
            mx_pass(acc, n, t, 0, False)

        weights(2, (("vector", 0, 2), ("scalar", 2, 4)))
        edge_features(1, "vector")
        edge_features(2, "vector")

        h_span = [sb.tile([P, hi - lo, PACK], BF16, name=f"h{lo}", align_bytes=64) for lo, hi in SPANS]
        h_planes = sb.tile([P, PACK, SPANS[0][1]], BF16, name="h_planes")
        for t in range(PACK):
            mx_pass(wide[t][:], 0, t, 2, False)
            nc.scalar.activation(out=h_planes[:, t, :], in_=wide[t][:], func=SILU)
        for n in (1, 2):
            mx_pass(narrow[n][:, 0, :], n, 0, 2, False)
            for t in range(1, PACK):
                for i in range(3):
                    mx_pass(narrow[n][:, t, :], n, t, i, i == 0)
            nc.scalar.activation(out=h_span[n][:], in_=narrow[n][:].rearrange("p t v -> p v t"), func=SILU)

        w4_grouped = sb.tile([P, N, PACK], BF16, name="w4_grouped", align_bytes=64)
        cast("vector", w4_grouped[:].rearrange("p (c i) t -> p c t i", i=4),
             w4_raw[:].rearrange("p t (c i) -> p c t i", i=4))
        w4_q = quantize("w4", w4_grouped[:].rearrange("p c t -> p (c t)"), N)
        nc.vector.tensor_copy(out=h_span[0][:].rearrange("p (c i) t -> p c t i", i=4),
                              in_=h_planes[:].rearrange("p t (c i) -> p c t i", i=4))

        out_rows = out.rearrange("(a p) v -> p a v", p=P)
        for n, (lo, hi) in enumerate(SPANS):
            width = hi - lo
            h_q = quantize(f"h{lo}", h_span[n][:].rearrange("p v t -> p (v t)"), width)
            groups = (((0, 1, 6, "vector"), (1, 2, 7, "scalar")), ((0, 2, 1, "scalar"),), ((0, 2, 0, "vector"),))[n]
            for a0, a1, bank, engine in groups:
                res = ps.tile([P, a1 - a0, width], F32, name=f"res{lo}_{a0}", tag=f"bank{bank}")
                for a in range(a0, a1):
                    nc.tensor.matmul_mx(out=res[:, a - a0, :], lhsT=w4_q[0][:, a * P:(a + 1) * P].bitcast(FP8X4),
                                        lhsT_scale=w4_q[1][:, a * P:(a + 1) * P],
                                        rhs=h_q[0][:].bitcast(FP8X4), rhs_scale=h_q[1][:], start=True, stop=True)
                staged = sb.tile([P, a1 - a0, width], F32, name=f"staged{lo}_{a0}")
                cast(engine, staged[:], res[:])
                nc.sync.dma_start(out=out_rows[:, a0:a1, lo:hi], in_=staged[:])
